import numpy as np
import ml_dtypes


def mxq(x, axis, fmt="e4m3"):
    dtype, down = {"e4m3": (ml_dtypes.float8_e4m3fn, 7), "e5m2": (ml_dtypes.float8_e5m2, 14)}[fmt]
    v = np.moveaxis(np.asarray(x, np.float32).astype(ml_dtypes.bfloat16).astype(np.float64), axis, -1)
    blocks = v.reshape(v.shape[:-1] + (-1, 32))
    amax = np.abs(blocks).max(-1, keepdims=True)
    byte = np.maximum(np.where(amax > 0, np.frexp(amax)[1] - 1 + 127, 0) - down, 1)
    scale = np.exp2(byte - 127.0)
    codes = (blocks / scale).astype(np.float32).astype(dtype).astype(np.float64)
    return np.moveaxis((codes * scale).reshape(v.shape), -1, axis)


WIDE = False


def mx_kscale(k):
    if not WIDE:
        return np.ones(k)
    levels = np.array([10, -10, 5, -5, 0])
    if k % 512:
        return np.exp2(np.random.permutation(np.resize(levels, k // 32))).repeat(32)
    a = np.empty((k // 512, 16))
    for p in range(k // 512):
        a[p, :8] = np.random.permutation(np.resize(levels, 8))
        for g in range(8):
            far = levels[np.abs(levels - a[p, g]) >= 10]
            a[p, g + 8] = far[np.random.randint(len(far))]
    return np.exp2(a.ravel()).repeat(32)


def f64(x):
    return np.asarray(x).astype(np.float64)


def striped8(idx):
    return np.asarray(idx).reshape(8, -1, 16).transpose(0, 2, 1).reshape(128, -1).astype(np.uint16)


def unstriped8(offs):
    return offs.reshape(8, 16, -1).transpose(0, 2, 1).reshape(8, -1).astype(np.int64)


def pick8(x, idx, run):
    r = np.arange(len(x))
    return x[r[:, None], idx[r % (8 * run) // run]]


E2M1 = np.array([0.0, 0.5, 1.0, 1.5, 2.0, 3.0, 4.0, 6.0, -0.0, -0.5, -1.0, -1.5, -2.0, -3.0, -4.0, -6.0])


def pack_weight(w, fmt):
    k, n = w.shape
    w = f64(np.asarray(w, np.float32).astype(ml_dtypes.bfloat16)).reshape(k // 32, 32, n)
    amax = np.abs(w).max(1)
    if fmt == "e4m3":
        byte = np.frexp(amax)[1] - 1 + 127 - 7
    else:
        mant, ex = np.frexp(amax / 6.0)
        byte = np.where(mant > 0.5, ex, ex - 1) + 127
    byte = np.clip(np.where(amax > 0, byte, 1), 1, 254)
    scaled = (w * np.exp2(127.0 - byte)[:, None, :]).reshape(k, n).astype(np.float32)
    by_word = np.ascontiguousarray(scaled.reshape(k // 512, 128, 4, n).transpose(0, 1, 3, 2))
    if fmt == "e4m3":
        words = by_word.astype(ml_dtypes.float8_e4m3fn).view(np.uint8)
    else:
        c = by_word.astype(ml_dtypes.float4_e2m1fn).view(np.uint8) & 0xF
        words = (c[..., 0::2] | (c[..., 1::2] << 4)).reshape(k // 512, 128, 2 * n)
    return np.ascontiguousarray(words), np.ascontiguousarray(byte.astype(np.uint8).reshape(k // 512, 16, n))


def unpack_weight(words, scales, fmt):
    g, _, n = scales.shape
    words = np.ascontiguousarray(words).reshape(g, 128, n, -1)
    if fmt == "e4m3":
        vals = words.view(ml_dtypes.float8_e4m3fn).astype(np.float64)
    else:
        nib = np.empty((g, 128, n, 4), np.uint8)
        nib[..., 0::2] = words & 0xF
        nib[..., 1::2] = words >> 4
        vals = E2M1[nib]
    vals = vals * np.repeat(np.exp2(scales.astype(np.float64) - 127.0), 8, axis=1)[..., None]
    return vals.transpose(0, 1, 3, 2).reshape(g * 512, n)


D, T, I, Q = 512, 1024, 512, 128


def setup_inputs():
    n = np.random.standard_normal
    idx = np.stack([np.random.permutation(T)[:I] for _ in range(8)])
    idx2 = np.stack([np.random.permutation(T)[:I] for _ in range(8)])
    idx3 = np.stack([np.random.permutation(T)[:I] for _ in range(8)])
    fd = mx_kscale(D)
    keysp = pack_weight(n((D, T)) / fd[:, None], "e4m3")
    return {
        "query": (n((D, Q)) * 0.9 / np.sqrt(D) * fd[:, None]).astype(np.float32),
        "query2": (n((D, Q)) * 0.9 / np.sqrt(D) * fd[:, None]).astype(np.float32),
        "keys_words": keysp[0],
        "keys_scales": keysp[1],
        "lam": (np.random.uniform(0.5, 1.3, (Q, 1))).astype(np.float32),
        "old": (1.0 * n((Q, T))).astype(np.float32),
        "offs": striped8(idx),
        "offs2": striped8(idx2),
        "offs3": striped8(idx3),
    }


def reference(query, query2, keys_words, keys_scales, lam, old, offs, offs2, offs3):
    idx = unstriped8(offs)
    idx2 = unstriped8(offs2)
    idx3 = unstriped8(offs3)
    keysu = unpack_weight(keys_words, keys_scales, "e4m3")
    queryq = mxq(f64(query), 0, "e4m3")
    a = queryq.T @ keysu
    query2q = mxq(f64(query2), 0, "e4m3")
    b = query2q.T @ keysu
    w = (np.maximum(pick8(a, idx, 16), pick8(b, idx2, 16)) - np.maximum(pick8(a, idx2, 16), pick8(b, idx, 16))) * f64(lam)
    f1 = np.zeros((Q, T))
    f1[np.arange(Q)[:, None], idx3[np.arange(Q) % 128 // 16]] = w
    y = f64(old) + f1
    return y

@@ -1,0 +1,135 @@
+from contextlib import ExitStack
+
+import concourse.mybir as mybir
+
+D, T, SLOTS, Q = 512, 1024, 512, 128
+FLOPS = 2 * 2 * D * Q * T
+
+F32 = mybir.dt.float32
+BF16 = mybir.dt.bfloat16
+I32 = mybir.dt.int32
+U32 = mybir.dt.uint32
+U16 = mybir.dt.uint16
+U8 = mybir.dt.uint8
+FP8X4 = mybir.dt.float8_e4m3fn_x4
+ALU = mybir.AluOpType
+COPY = mybir.ActivationFunctionType.Copy
+
+P = 128
+PACK = 4
+KEY_LOAD = 512
+N_MM = 256
+HALF = SLOTS // 2
+LIST_COLS = HALF // 16
+STORE = 256
+
+
+def tile_attend_exchanged_lean_putold_heads_kernel(
+    tc, query, query2, keys_words, keys_scales, lam, old, offs, offs2, offs3, out
+):
+    nc = tc.nc
+    with ExitStack() as ctx:
+        keep = ctx.enter_context(tc.tile_pool(name="keep", bufs=1))
+        psum = ctx.enter_context(tc.psum_pool(name="psum", bufs=1))
+
+        idx1 = keep.tile([P, SLOTS // 16], U16, name="idx1")
+        idx2 = keep.tile([P, SLOTS // 16], U16, name="idx2")
+        idx3 = keep.tile([P, SLOTS // 16], U16, name="idx3")
+
+        key_scales = keep.tile([P, T], U8, name="key_scales", align_bytes=64)
+        nc.vector.memset(key_scales[:].bitcast(I32), 0)
+        placed = keep.tile([P, T], F32, name="placed")
+        nc.vector.memset(placed[:], 0.0)
+
+        raw = [keep.tile([P, PACK, Q], F32, name="raw%d" % s) for s in range(2)]
+        key_words = [keep.tile([P, KEY_LOAD], U32, name="key_words%d" % c, align_bytes=64) for c in range(2)]
+        words_hbm = keys_words[0].rearrange("p n t -> p (n t)")
+
+        def load_query(s, src):
+            nc.sync.dma_start(out=raw[s][:], in_=src.rearrange("(p j) q -> p j q", j=PACK))
+
+        def load_keys(c):
+            nc.sync.dma_start(
+                out=key_words[c][:].bitcast(I32),
+                in_=words_hbm[:, c * KEY_LOAD * PACK : (c + 1) * KEY_LOAD * PACK].bitcast(I32),
+            )
+
+        load_query(0, query)
+        for quad in range(4):
+            nc.sync.dma_start(
+                out=key_scales[32 * quad : 32 * quad + 4, :].bitcast(I32),
+                in_=keys_scales[0][4 * quad : 4 * quad + 4, :].bitcast(I32),
+            )
+        load_keys(0)
+        load_query(1, query2)
+        load_keys(1)
+        nc.sync.dma_start(idx1[:], offs)
+        nc.sync.dma_start(idx2[:], offs2)
+        lam_col = keep.tile([P, 1], F32, name="lam_col")
+        nc.sync.dma_start(out=lam_col[:], in_=lam)
+        nc.sync.dma_start(idx3[:], offs3)
+        total = keep.tile([P, T], F32, name="total")
+        nc.sync.dma_start(out=total[:], in_=old)
+
+        codes, scales = [], []
+        for s in range(2):
+            grouped = keep.tile([P, Q, PACK], BF16, name="grouped%d" % s, align_bytes=64)
+            nc.vector.tensor_copy(
+                out=grouped[:].rearrange("p (c i) j -> p c j i", i=4),
+                in_=raw[s][:].rearrange("p j (c i) -> p c j i", i=4),
+            )
+            code = keep.tile([P, Q], U32, name="codes%d" % s, align_bytes=64)
+            scale = keep.tile([P, Q], U8, name="scales%d" % s, align_bytes=64)
+            nc.vector.quantize_mx(
+                out=code[:].bitcast(FP8X4), scales=scale[:], in_=grouped[:].rearrange("p q j -> p (q j)")
+            )
+            codes.append(code)
+            scales.append(scale)
+
+        lam_wide = keep.tile([P, HALF], F32, name="lam_wide")
+        ones = keep.tile([P, HALF], F32, name="ones")
+        nc.gpsimd.memset(ones[:], 1.0)
+        nc.gpsimd.tensor_scalar(lam_wide[:], ones[:], lam_col[:, 0:1], 0.0, ALU.mult, ALU.add)
+
+        scores = [keep.tile([P, T], F32, name="scores%d" % s) for s in range(2)]
+        for s in range(2):
+            for n0 in range(0, T, N_MM):
+                c, w0 = divmod(n0, KEY_LOAD)
+                bank = psum.tile([P, N_MM], F32, name="bank%d_%d" % (s, n0))
+                nc.tensor.matmul_mx(
+                    out=bank[:],
+                    lhsT=codes[s][:].bitcast(FP8X4),
+                    lhsT_scale=scales[s][:],
+                    rhs=key_words[c][:, w0 : w0 + N_MM].bitcast(FP8X4),
+                    rhs_scale=key_scales[:, n0 : n0 + N_MM],
+                    start=True,
+                    stop=True,
+                )
+                nc.scalar.copy(out=scores[s][:, n0 : n0 + N_MM], in_=bank[:])
+        a, b = scores
+
+        def on_vector(dst, window, offsets):
+            nc.vector.tensor_copy(dst, window[:].indirect(offsets))
+
+        def on_scalar(dst, window, offsets):
+            nc.scalar.activation(dst, window[:].indirect(offsets), COPY)
+
+        for h in range(2):
+            cols = slice(h * LIST_COLS, (h + 1) * LIST_COLS)
+            from_a = keep.tile([P, 2, HALF], F32, name="from_a%d" % h)
+            from_b = keep.tile([P, 2, HALF], F32, name="from_b%d" % h)
+            first = on_vector if h == 0 else on_scalar
+            first(from_a[:, 0, :], a, idx1[:, cols])
+            first(from_a[:, 1, :], a, idx2[:, cols])
+            on_scalar(from_b[:, 0, :], b, idx2[:, cols])
+            first(from_b[:, 1, :], b, idx1[:, cols])
+            larger = keep.tile([P, 2, HALF], F32, name="larger%d" % h, tag="larger")
+            nc.vector.tensor_tensor(larger[:], from_a[:], from_b[:], ALU.max)
+            nc.vector.tensor_tensor(larger[:, 0, :], larger[:, 0, :], larger[:, 1, :], ALU.subtract)
+            nc.vector.tensor_tensor(placed[:].indirect(idx3[:, cols]), larger[:, 0, :], lam_wide[:], ALU.mult)
+
+        for c0 in range(0, T, STORE):
+            nc.vector.tensor_tensor(
+                total[:, c0 : c0 + STORE], total[:, c0 : c0 + STORE], placed[:, c0 : c0 + STORE], ALU.add
+            )
+            nc.sync.dma_start(out=out[:, c0 : c0 + STORE], in_=total[:, c0 : c0 + STORE])

@@ -55,18 +55,18 @@ def tile_attend_exchanged_lean_putold_heads_kernel(
             )
 
         load_query(0, query)
+        load_query(1, query2)
         for quad in range(4):
             nc.sync.dma_start(
                 out=key_scales[32 * quad : 32 * quad + 4, :].bitcast(I32),
                 in_=keys_scales[0][4 * quad : 4 * quad + 4, :].bitcast(I32),
             )
         load_keys(0)
-        load_query(1, query2)
         load_keys(1)
         nc.sync.dma_start(idx1[:], offs)
-        nc.sync.dma_start(idx2[:], offs2)
         lam_col = keep.tile([P, 1], F32, name="lam_col")
         nc.sync.dma_start(out=lam_col[:], in_=lam)
+        nc.sync.dma_start(idx2[:], offs2)
         nc.sync.dma_start(idx3[:], offs3)
         total = keep.tile([P, T], F32, name="total")
         nc.sync.dma_start(out=total[:], in_=old)
@@ -74,10 +74,13 @@ def tile_attend_exchanged_lean_putold_heads_kernel(
         codes, scales = [], []
         for s in range(2):
             grouped = keep.tile([P, Q, PACK], BF16, name="grouped%d" % s, align_bytes=64)
-            nc.vector.tensor_copy(
-                out=grouped[:].rearrange("p (c i) j -> p c j i", i=4),
-                in_=raw[s][:].rearrange("p j (c i) -> p c j i", i=4),
-            )
+            split = Q // 2 if s == 0 else 0
+            for copy, q0, q1 in ((nc.vector.tensor_copy, 0, split), (nc.scalar.copy, split, Q)):
+                if q1 > q0:
+                    copy(
+                        out=grouped[:, q0:q1, :].rearrange("p (c i) j -> p c j i", i=4),
+                        in_=raw[s][:, :, q0:q1].rearrange("p j (c i) -> p c j i", i=4),
+                    )
             code = keep.tile([P, Q], U32, name="codes%d" % s, align_bytes=64)
             scale = keep.tile([P, Q], U8, name="scales%d" % s, align_bytes=64)
             nc.vector.quantize_mx(
@@ -105,7 +108,8 @@ def tile_attend_exchanged_lean_putold_heads_kernel(
                     start=True,
                     stop=True,
                 )
-                nc.scalar.copy(out=scores[s][:, n0 : n0 + N_MM], in_=bank[:])
+                copy = nc.vector.tensor_copy if s == 0 and n0 in (N_MM, 2 * N_MM) else nc.scalar.copy
+                copy(out=scores[s][:, n0 : n0 + N_MM], in_=bank[:])
         a, b = scores
 
         def on_vector(dst, window, offsets):
@@ -116,17 +120,25 @@ def tile_attend_exchanged_lean_putold_heads_kernel(
 
         for h in range(2):
             cols = slice(h * LIST_COLS, (h + 1) * LIST_COLS)
-            from_a = keep.tile([P, 2, HALF], F32, name="from_a%d" % h)
+            from_a = keep.tile([P, 2, HALF], F32, name="from_a%d" % h, tag="from_a")
             from_b = keep.tile([P, 2, HALF], F32, name="from_b%d" % h)
             first = on_vector if h == 0 else on_scalar
-            first(from_a[:, 0, :], a, idx1[:, cols])
-            first(from_a[:, 1, :], a, idx2[:, cols])
+            if h == 0:
+                first(from_a[:, 0, :], a, idx1[:, cols])
+                first(from_a[:, 1, :], a, idx2[:, cols])
             on_scalar(from_b[:, 0, :], b, idx2[:, cols])
             first(from_b[:, 1, :], b, idx1[:, cols])
+            if h == 1:
+                first(from_a[:, 0, :], a, idx1[:, cols])
+                first(from_a[:, 1, :], a, idx2[:, cols])
             larger = keep.tile([P, 2, HALF], F32, name="larger%d" % h, tag="larger")
-            nc.vector.tensor_tensor(larger[:], from_a[:], from_b[:], ALU.max)
-            nc.vector.tensor_tensor(larger[:, 0, :], larger[:, 0, :], larger[:, 1, :], ALU.subtract)
-            nc.vector.tensor_tensor(placed[:].indirect(idx3[:, cols]), larger[:, 0, :], lam_wide[:], ALU.mult)
+            diff = keep.tile([P, HALF], F32, name="diff%d" % h)
+            pieces = [slice(0, HALF // 2), slice(HALF // 2, HALF)]
+            for piece in pieces:
+                nc.vector.tensor_tensor(larger[:, :, piece], from_a[:, :, piece], from_b[:, :, piece], ALU.max)
+            for piece in pieces:
+                nc.vector.tensor_tensor(diff[:, piece], larger[:, 0, piece], larger[:, 1, piece], ALU.subtract)
+            nc.vector.tensor_tensor(placed[:].indirect(idx3[:, cols]), diff[:], lam_wide[:], ALU.mult)
 
         for c0 in range(0, T, STORE):
             nc.vector.tensor_tensor(

@@ -30,7 +30,7 @@ def tile_attend_exchanged_lean_putold_heads_kernel(
     nc = tc.nc
     with ExitStack() as ctx:
         keep = ctx.enter_context(tc.tile_pool(name="keep", bufs=1))
-        psum = ctx.enter_context(tc.psum_pool(name="psum", bufs=1))
+        psum = ctx.enter_context(tc.psum_pool(name="psum", bufs=4))
 
         idx1 = keep.tile([P, SLOTS // 16], U16, name="idx1")
         idx2 = keep.tile([P, SLOTS // 16], U16, name="idx2")
@@ -98,7 +98,7 @@ def tile_attend_exchanged_lean_putold_heads_kernel(
         for s in range(2):
             for n0 in range(0, T, N_MM):
                 c, w0 = divmod(n0, KEY_LOAD)
-                bank = psum.tile([P, N_MM], F32, name="bank%d_%d" % (s, n0))
+                bank = psum.tile([P, N_MM], F32, name="bank%d_%d" % (s, n0), tag="bank")
                 nc.tensor.matmul_mx(
                     out=bank[:],
                     lhsT=codes[s][:].bitcast(FP8X4),
@@ -118,26 +118,31 @@ def tile_attend_exchanged_lean_putold_heads_kernel(
         def on_scalar(dst, window, offsets):
             nc.scalar.activation(dst, window[:].indirect(offsets), COPY)
 
+        pieces = [slice(0, HALF // 2), slice(HALF // 2, HALF)]
         for h in range(2):
             cols = slice(h * LIST_COLS, (h + 1) * LIST_COLS)
-            from_a = keep.tile([P, 2, HALF], F32, name="from_a%d" % h, tag="from_a")
-            from_b = keep.tile([P, 2, HALF], F32, name="from_b%d" % h)
-            first = on_vector if h == 0 else on_scalar
-            if h == 0:
-                first(from_a[:, 0, :], a, idx1[:, cols])
-                first(from_a[:, 1, :], a, idx2[:, cols])
-            on_scalar(from_b[:, 0, :], b, idx2[:, cols])
-            first(from_b[:, 1, :], b, idx1[:, cols])
-            if h == 1:
-                first(from_a[:, 0, :], a, idx1[:, cols])
-                first(from_a[:, 1, :], a, idx2[:, cols])
-            larger = keep.tile([P, 2, HALF], F32, name="larger%d" % h, tag="larger")
+            a1 = keep.tile([P, HALF], F32, name="a1_%d" % h, tag="a1")
+            a2 = keep.tile([P, HALF], F32, name="a2_%d" % h, tag="a2")
+            b1 = keep.tile([P, HALF], F32, name="b1_%d" % h)
+            b2 = keep.tile([P, HALF], F32, name="b2_%d" % h)
+            kept = keep.tile([P, HALF], F32, name="kept%d" % h, tag="kept")
+            exchanged = keep.tile([P, HALF], F32, name="exchanged%d" % h, tag="exchanged")
             diff = keep.tile([P, HALF], F32, name="diff%d" % h)
-            pieces = [slice(0, HALF // 2), slice(HALF // 2, HALF)]
+            if h == 0:
+                on_vector(a1[:], a, idx1[:, cols])
+                on_vector(a2[:], a, idx2[:, cols])
+                on_scalar(b2[:], b, idx2[:, cols])
+                on_vector(b1[:], b, idx1[:, cols])
+            else:
+                on_scalar(b2[:], b, idx2[:, cols])
+                on_scalar(b1[:], b, idx1[:, cols])
+                on_scalar(a1[:], a, idx1[:, cols])
+                on_scalar(a2[:], a, idx2[:, cols])
+            nc.vector.tensor_tensor(kept[:], a1[:], b2[:], ALU.max)
             for piece in pieces:
-                nc.vector.tensor_tensor(larger[:, :, piece], from_a[:, :, piece], from_b[:, :, piece], ALU.max)
+                nc.vector.tensor_tensor(exchanged[:, piece], a2[:, piece], b1[:, piece], ALU.max)
             for piece in pieces:
-                nc.vector.tensor_tensor(diff[:, piece], larger[:, 0, piece], larger[:, 1, piece], ALU.subtract)
+                nc.vector.tensor_tensor(diff[:, piece], kept[:, piece], exchanged[:, piece], ALU.subtract)
             nc.vector.tensor_tensor(placed[:].indirect(idx3[:, cols]), diff[:], lam_wide[:], ALU.mult)
 
         for c0 in range(0, T, STORE):

@@ -36,7 +36,7 @@ def tile_attend_exchanged_lean_putold_heads_kernel(
         idx2 = keep.tile([P, SLOTS // 16], U16, name="idx2")
         idx3 = keep.tile([P, SLOTS // 16], U16, name="idx3")
 
-        key_scales = keep.tile([P, T], U8, name="key_scales", align_bytes=64)
+        key_scales = keep.tile([P, N_MM], U8, name="key_scales", align_bytes=64)
         nc.vector.memset(key_scales[:].bitcast(I32), 0)
         placed = keep.tile([P, T], F32, name="placed")
         nc.vector.memset(placed[:], 0.0)
@@ -58,8 +58,8 @@ def tile_attend_exchanged_lean_putold_heads_kernel(
         load_query(1, query2)
         for quad in range(4):
             nc.sync.dma_start(
-                out=key_scales[32 * quad : 32 * quad + 4, :].bitcast(I32),
-                in_=keys_scales[0][4 * quad : 4 * quad + 4, :].bitcast(I32),
+                out=key_scales[32 * quad : 32 * quad + 16, :].bitcast(I32),
+                in_=keys_scales[0][4 * quad : 4 * quad + 4, :].bitcast(I32).rearrange("r (c w) -> c r w", c=4),
             )
         load_keys(0)
         load_keys(1)
@@ -104,7 +104,7 @@ def tile_attend_exchanged_lean_putold_heads_kernel(
                     lhsT=codes[s][:].bitcast(FP8X4),
                     lhsT_scale=scales[s][:],
                     rhs=key_words[c][:, w0 : w0 + N_MM].bitcast(FP8X4),
-                    rhs_scale=key_scales[:, n0 : n0 + N_MM],
+                    rhs_scale=key_scales[4 * (n0 // N_MM) : P, :],
                     start=True,
                     stop=True,
                 )

from contextlib import ExitStack

import concourse.mybir as mybir

D, T, SLOTS, Q = 512, 1024, 512, 128
FLOPS = 2 * 2 * D * Q * T

F32 = mybir.dt.float32
BF16 = mybir.dt.bfloat16
I32 = mybir.dt.int32
U32 = mybir.dt.uint32
U16 = mybir.dt.uint16
U8 = mybir.dt.uint8
FP8X4 = mybir.dt.float8_e4m3fn_x4
ALU = mybir.AluOpType
COPY = mybir.ActivationFunctionType.Copy

P = 128
PACK = 4
KEY_LOAD = 512
N_MM = 256
HALF = SLOTS // 2
LIST_COLS = HALF // 16
STORE = 256


def tile_attend_exchanged_lean_putold_heads_kernel(
    tc, query, query2, keys_words, keys_scales, lam, old, offs, offs2, offs3, out
):
    nc = tc.nc
    with ExitStack() as ctx:
        keep = ctx.enter_context(tc.tile_pool(name="keep", bufs=1))
        psum = ctx.enter_context(tc.psum_pool(name="psum", bufs=4))

        idx1 = keep.tile([P, SLOTS // 16], U16, name="idx1")
        idx2 = keep.tile([P, SLOTS // 16], U16, name="idx2")
        idx3 = keep.tile([P, SLOTS // 16], U16, name="idx3")

        key_scales = keep.tile([P, N_MM], U8, name="key_scales", align_bytes=64)
        nc.vector.memset(key_scales[:].bitcast(I32), 0)
        placed = keep.tile([P, T], F32, name="placed")
        nc.vector.memset(placed[:], 0.0)

        raw = [keep.tile([P, PACK, Q], F32, name="raw%d" % s) for s in range(2)]
        key_words = [keep.tile([P, KEY_LOAD], U32, name="key_words%d" % c, align_bytes=64) for c in range(2)]
        words_hbm = keys_words[0].rearrange("p n t -> p (n t)")

        def load_query(s, src):
            nc.sync.dma_start(out=raw[s][:], in_=src.rearrange("(p j) q -> p j q", j=PACK))

        def load_keys(c):
            nc.sync.dma_start(
                out=key_words[c][:].bitcast(I32),
                in_=words_hbm[:, c * KEY_LOAD * PACK : (c + 1) * KEY_LOAD * PACK].bitcast(I32),
            )

        load_query(0, query)
        load_query(1, query2)
        for quad in range(4):
            nc.sync.dma_start(
                out=key_scales[32 * quad : 32 * quad + 16, :].bitcast(I32),
                in_=keys_scales[0][4 * quad : 4 * quad + 4, :].bitcast(I32).rearrange("r (c w) -> c r w", c=4),
            )
        load_keys(0)
        load_keys(1)
        nc.sync.dma_start(idx1[:], offs)
        lam_col = keep.tile([P, 1], F32, name="lam_col")
        nc.sync.dma_start(out=lam_col[:], in_=lam)
        nc.sync.dma_start(idx2[:], offs2)
        nc.sync.dma_start(idx3[:], offs3)
        total = keep.tile([P, T], F32, name="total")
        nc.sync.dma_start(out=total[:], in_=old)

        codes, scales = [], []
        for s in range(2):
            grouped = keep.tile([P, Q, PACK], BF16, name="grouped%d" % s, align_bytes=64)
            split = Q // 2 if s == 0 else 0
            for copy, q0, q1 in ((nc.vector.tensor_copy, 0, split), (nc.scalar.copy, split, Q)):
                if q1 > q0:
                    copy(
                        out=grouped[:, q0:q1, :].rearrange("p (c i) j -> p c j i", i=4),
                        in_=raw[s][:, :, q0:q1].rearrange("p j (c i) -> p c j i", i=4),
                    )
            code = keep.tile([P, Q], U32, name="codes%d" % s, align_bytes=64)
            scale = keep.tile([P, Q], U8, name="scales%d" % s, align_bytes=64)
            nc.vector.quantize_mx(
                out=code[:].bitcast(FP8X4), scales=scale[:], in_=grouped[:].rearrange("p q j -> p (q j)")
            )
            codes.append(code)
            scales.append(scale)

        lam_wide = keep.tile([P, HALF], F32, name="lam_wide")
        ones = keep.tile([P, HALF], F32, name="ones")
        nc.gpsimd.memset(ones[:], 1.0)
        nc.gpsimd.tensor_scalar(lam_wide[:], ones[:], lam_col[:, 0:1], 0.0, ALU.mult, ALU.add)

        scores = [keep.tile([P, T], F32, name="scores%d" % s) for s in range(2)]
        for s in range(2):
            for n0 in range(0, T, N_MM):
                c, w0 = divmod(n0, KEY_LOAD)
                bank = psum.tile([P, N_MM], F32, name="bank%d_%d" % (s, n0), tag="bank")
                nc.tensor.matmul_mx(
                    out=bank[:],
                    lhsT=codes[s][:].bitcast(FP8X4),
                    lhsT_scale=scales[s][:],
                    rhs=key_words[c][:, w0 : w0 + N_MM].bitcast(FP8X4),
                    rhs_scale=key_scales[4 * (n0 // N_MM) : P, :],
                    start=True,
                    stop=True,
                )
                copy = nc.vector.tensor_copy if s == 0 and n0 in (N_MM, 2 * N_MM) else nc.scalar.copy
                copy(out=scores[s][:, n0 : n0 + N_MM], in_=bank[:])
        a, b = scores

        def on_vector(dst, window, offsets):
            nc.vector.tensor_copy(dst, window[:].indirect(offsets))

        def on_scalar(dst, window, offsets):
            nc.scalar.activation(dst, window[:].indirect(offsets), COPY)

        pieces = [slice(0, HALF // 2), slice(HALF // 2, HALF)]
        for h in range(2):
            cols = slice(h * LIST_COLS, (h + 1) * LIST_COLS)
            a1 = keep.tile([P, HALF], F32, name="a1_%d" % h, tag="a1")
            a2 = keep.tile([P, HALF], F32, name="a2_%d" % h, tag="a2")
            b1 = keep.tile([P, HALF], F32, name="b1_%d" % h)
            b2 = keep.tile([P, HALF], F32, name="b2_%d" % h)
            kept = keep.tile([P, HALF], F32, name="kept%d" % h, tag="kept")
            exchanged = keep.tile([P, HALF], F32, name="exchanged%d" % h, tag="exchanged")
            diff = keep.tile([P, HALF], F32, name="diff%d" % h)
            if h == 0:
                on_vector(a1[:], a, idx1[:, cols])
                on_vector(a2[:], a, idx2[:, cols])
                on_scalar(b2[:], b, idx2[:, cols])
                on_vector(b1[:], b, idx1[:, cols])
            else:
                on_scalar(b2[:], b, idx2[:, cols])
                on_scalar(b1[:], b, idx1[:, cols])
                on_scalar(a1[:], a, idx1[:, cols])
                on_scalar(a2[:], a, idx2[:, cols])
            nc.vector.tensor_tensor(kept[:], a1[:], b2[:], ALU.max)
            for piece in pieces:
                nc.vector.tensor_tensor(exchanged[:, piece], a2[:, piece], b1[:, piece], ALU.max)
            for piece in pieces:
                nc.vector.tensor_tensor(diff[:, piece], kept[:, piece], exchanged[:, piece], ALU.subtract)
            nc.vector.tensor_tensor(placed[:].indirect(idx3[:, cols]), diff[:], lam_wide[:], ALU.mult)

        for c0 in range(0, T, STORE):
            nc.vector.tensor_tensor(
                total[:, c0 : c0 + STORE], total[:, c0 : c0 + STORE], placed[:, c0 : c0 + STORE], ALU.add
            )
            nc.sync.dma_start(out=out[:, c0 : c0 + STORE], in_=total[:, c0 : c0 + STORE])
